import numpy as np
import ml_dtypes


def mxq(x, axis, fmt="e4m3"):
    dtype, down = {"e4m3": (ml_dtypes.float8_e4m3fn, 7), "e5m2": (ml_dtypes.float8_e5m2, 14)}[fmt]
    v = np.moveaxis(np.asarray(x, np.float32).astype(ml_dtypes.bfloat16).astype(np.float64), axis, -1)
    blocks = v.reshape(v.shape[:-1] + (-1, 32))
    amax = np.abs(blocks).max(-1, keepdims=True)
    byte = np.maximum(np.where(amax > 0, np.frexp(amax)[1] - 1 + 127, 0) - down, 1)
    scale = np.exp2(byte - 127.0)
    codes = (blocks / scale).astype(np.float32).astype(dtype).astype(np.float64)
    return np.moveaxis((codes * scale).reshape(v.shape), -1, axis)


WIDE = False


def mx_kscale(k):
    if not WIDE:
        return np.ones(k)
    levels = np.array([10, -10, 5, -5, 0])
    if k % 512:
        return np.exp2(np.random.permutation(np.resize(levels, k // 32))).repeat(32)
    a = np.empty((k // 512, 16))
    for p in range(k // 512):
        a[p, :8] = np.random.permutation(np.resize(levels, 8))
        for g in range(8):
            far = levels[np.abs(levels - a[p, g]) >= 10]
            a[p, g + 8] = far[np.random.randint(len(far))]
    return np.exp2(a.ravel()).repeat(32)


def f64(x):
    return np.asarray(x).astype(np.float64)


def striped(idx):
    return np.tile(np.asarray(idx).reshape(-1, 16).T, (8, 1)).astype(np.uint16)


def unstriped(offs):
    return offs[:16].T.reshape(-1).astype(np.int64)


def striped8(idx):
    return np.asarray(idx).reshape(8, -1, 16).transpose(0, 2, 1).reshape(128, -1).astype(np.uint16)


def unstriped8(offs):
    return offs.reshape(8, 16, -1).transpose(0, 2, 1).reshape(8, -1).astype(np.int64)


def pick8(x, idx, run):
    r = np.arange(len(x))
    return x[r[:, None], idx[r % (8 * run) // run]]


E2M1 = np.array([0.0, 0.5, 1.0, 1.5, 2.0, 3.0, 4.0, 6.0, -0.0, -0.5, -1.0, -1.5, -2.0, -3.0, -4.0, -6.0])


def pack_weight(w, fmt):
    k, n = w.shape
    w = f64(np.asarray(w, np.float32).astype(ml_dtypes.bfloat16)).reshape(k // 32, 32, n)
    amax = np.abs(w).max(1)
    if fmt == "e4m3":
        byte = np.frexp(amax)[1] - 1 + 127 - 7
    else:
        mant, ex = np.frexp(amax / 6.0)
        byte = np.where(mant > 0.5, ex, ex - 1) + 127
    byte = np.clip(np.where(amax > 0, byte, 1), 1, 254)
    scaled = (w * np.exp2(127.0 - byte)[:, None, :]).reshape(k, n).astype(np.float32)
    by_word = np.ascontiguousarray(scaled.reshape(k // 512, 128, 4, n).transpose(0, 1, 3, 2))
    if fmt == "e4m3":
        words = by_word.astype(ml_dtypes.float8_e4m3fn).view(np.uint8)
    else:
        c = by_word.astype(ml_dtypes.float4_e2m1fn).view(np.uint8) & 0xF
        words = (c[..., 0::2] | (c[..., 1::2] << 4)).reshape(k // 512, 128, 2 * n)
    return np.ascontiguousarray(words), np.ascontiguousarray(byte.astype(np.uint8).reshape(k // 512, 16, n))


def unpack_weight(words, scales, fmt):
    g, _, n = scales.shape
    words = np.ascontiguousarray(words).reshape(g, 128, n, -1)
    if fmt == "e4m3":
        vals = words.view(ml_dtypes.float8_e4m3fn).astype(np.float64)
    else:
        nib = np.empty((g, 128, n, 4), np.uint8)
        nib[..., 0::2] = words & 0xF
        nib[..., 1::2] = words >> 4
        vals = E2M1[nib]
    vals = vals * np.repeat(np.exp2(scales.astype(np.float64) - 127.0), 8, axis=1)[..., None]
    return vals.transpose(0, 1, 3, 2).reshape(g * 512, n)


def sigmoid(v):
    return 1.0 / (1.0 + np.exp(-v))


K, R, F, T, J, M = 512, 128, 512, 2048, 512, 256


def setup_inputs():
    n = np.random.standard_normal
    idx = np.random.permutation(T)[:J]
    idx4 = np.random.permutation(T)[:J]
    idx2 = np.stack([np.random.permutation(J)[:M] for _ in range(8)])
    idx3 = np.stack([np.random.permutation(J)[:M] for _ in range(8)])
    fk = mx_kscale(K)
    ff = mx_kscale(F)
    tabp = pack_weight(n((K, T)) / fk[:, None], "e2m1")
    tab2p = pack_weight(n((K, T)) / fk[:, None], "e2m1")
    return {
        "tab_words": tabp[0],
        "tab_scales": tabp[1],
        "w1": (n((K, R)) * 1 / np.sqrt(K) * fk[:, None]).astype(np.float32),
        "tab2_words": tab2p[0],
        "tab2_scales": tab2p[1],
        "w2": (n((K, R)) * 1 / np.sqrt(K) * fk[:, None]).astype(np.float32),
        "gain": (np.random.uniform(0.5, 1.5, (R, 1))).astype(np.float32),
        "wo": (n((F, R)) * 1 / np.sqrt(F) * ff[:, None]).astype(np.float32),
        "dy": (n((F, M)) / ff[:, None]).astype(np.float32),
        "og": (np.random.uniform(0.3, 1.0, (R, 1))).astype(np.float32),
        "base": (0.3 * n((R, J))).astype(np.float32),
        "offs": striped(idx),
        "offs4": striped(idx4),
        "offs2": striped8(idx2),
        "offs3": striped8(idx3),
    }


def reference(tab_words, tab_scales, w1, tab2_words, tab2_scales, w2, gain, wo, dy, og, base, offs, offs4, offs2, offs3):
    idx = unstriped(offs)
    idx4 = unstriped(offs4)
    idx2 = unstriped8(offs2)
    idx3 = unstriped8(offs3)
    tabu = unpack_weight(tab_words, tab_scales, "e2m1")
    tab2u = unpack_weight(tab2_words, tab2_scales, "e2m1")
    w1q = mxq(f64(w1), 0, "e4m3")
    tabidxg = tabu[:, idx]
    a = w1q.T @ tabidxg
    w2q = mxq(f64(w2), 0, "e4m3")
    tab2idx4g = tab2u[:, idx4]
    b = w2q.T @ tab2idx4g
    h0 = np.tanh(a)
    g1 = sigmoid(b)
    woq = mxq(f64(wo), 0, "e4m3")
    dyq = mxq(f64(dy), 0, "e4m3")
    c0 = woq.T @ dyq
    e1 = c0 * pick8(g1, idx3, 16)
    s1 = np.zeros((R, J))
    s1[np.arange(R)[:, None], idx2[np.arange(R) % 128 // 16]] = e1
    dh0 = s1 * f64(gain)
    da = dh0 * (1.0 - np.square(h0))
    hda = da * 2.0
    hh0 = hda * dh0 * (-1.0) * h0 * 2.0
    ha = hh0 * (1.0 - np.square(h0))
    y = ha * f64(og) + f64(base)
    return y

@@ -1,0 +1,162 @@
+from contextlib import ExitStack
+
+import concourse.mybir as mybir
+
+K, R, F, T, J, M = 512, 128, 512, 2048, 512, 256
+FLOPS = 2 * K * R * J * 2 + 2 * F * R * M
+
+F32 = mybir.dt.float32
+BF16 = mybir.dt.bfloat16
+I32 = mybir.dt.int32
+U32 = mybir.dt.uint32
+U16 = mybir.dt.uint16
+U8 = mybir.dt.uint8
+FP8X4 = mybir.dt.float8_e4m3fn_x4
+FP4X4 = mybir.dt.float4_e2m1fn_x4
+ACT = mybir.ActivationFunctionType
+ALU = mybir.AluOpType
+
+P = 128
+PACK = 4
+LINE = 4
+QUADS = 4
+HALVES = 2
+
+
+def interleave(nc, grouped, raw):
+    nc.scalar.copy(
+        out=grouped.rearrange("p (c i t) -> p c t i", i=LINE, t=PACK),
+        in_=raw.rearrange("p t (c i) -> p c t i", i=LINE),
+    )
+
+
+def load_scale_rows(queue, plane, scales):
+    for q in range(QUADS):
+        queue.dma_start(
+            out=plane[32 * q : 32 * q + 4, :].bitcast(I32),
+            in_=scales[0, 4 * q : 4 * q + 4, :].bitcast(I32),
+        )
+
+
+def tile_attend_gpcpickgates_kernel(
+    tc, tab_words, tab_scales, w1, tab2_words, tab2_scales, w2, gain, wo, dy, og, base, offs, offs4, offs2, offs3, out
+):
+    nc = tc.nc
+    with ExitStack() as ctx:
+        sb = ctx.enter_context(tc.tile_pool(name="sb", bufs=1))
+        ps = ctx.enter_context(tc.psum_pool(name="ps", bufs=1))
+
+        list_a = sb.tile([P, J // 16], U16, name="list_a")
+        list_b = sb.tile([P, J // 16], U16, name="list_b")
+        list_put = sb.tile([P, M // 16], U16, name="list_put")
+        list_gate = sb.tile([P, M // 16], U16, name="list_gate")
+        words_a = sb.tile([P, T], U16, name="words_a", align_bytes=64)
+        words_b = sb.tile([P, T], U16, name="words_b", align_bytes=64)
+        plane_a = sb.tile([P, T], U8, name="plane_a", align_bytes=64)
+        plane_b = sb.tile([P, T], U8, name="plane_b", align_bytes=64)
+        w1_raw = sb.tile([P, PACK, R], F32, name="w1_raw")
+        w2_raw = sb.tile([P, PACK, R], F32, name="w2_raw")
+        wo_raw = sb.tile([P, PACK, R], F32, name="wo_raw")
+        dy_raw = sb.tile([P, PACK, M], F32, name="dy_raw")
+        base_sb = sb.tile([P, J], F32, name="base_sb")
+        gain_sb = sb.tile([P, 1], F32, name="gain_sb")
+        og_sb = sb.tile([P, 1], F32, name="og_sb")
+        placed = sb.tile([P, J], F32, name="placed")
+        warm_in = sb.tile([P, 1], F32, name="warm_in")
+        warm_out = sb.tile([P, 1], F32, name="warm_out")
+
+        nc.vector.memset(plane_b[:].bitcast(I32), 0)
+        nc.vector.memset(plane_a[:].bitcast(I32), 0)
+        nc.vector.memset(placed[:], 0.0)
+        nc.gpsimd.memset(warm_in[:], 0.0)
+
+        nc.sync.dma_start(list_b[:], offs4)
+        nc.sync.dma_start(out=words_b[:].bitcast(I32), in_=tab2_words[0].bitcast(I32))
+        load_scale_rows(nc.scalar, plane_b, tab2_scales)
+        nc.scalar.activation(out=warm_out[:], in_=warm_in[:], func=ACT.Sigmoid)
+        nc.sync.dma_start(out=w2_raw[:], in_=w2.rearrange("(p t) r -> p t r", t=PACK))
+        nc.sync.dma_start(out=wo_raw[:], in_=wo.rearrange("(p t) r -> p t r", t=PACK))
+        nc.sync.dma_start(out=dy_raw[:], in_=dy.rearrange("(p t) m -> p t m", t=PACK))
+        nc.sync.dma_start(out=words_a[:].bitcast(I32), in_=tab_words[0].bitcast(I32))
+        nc.sync.dma_start(list_a[:], offs)
+        load_scale_rows(nc.sync, plane_a, tab_scales)
+        nc.sync.dma_start(out=w1_raw[:], in_=w1.rearrange("(p t) r -> p t r", t=PACK))
+        nc.sync.dma_start(list_gate[:], offs3)
+        nc.sync.dma_start(list_put[:], offs2)
+        nc.sync.dma_start(out=base_sb[:], in_=base)
+        nc.gpsimd.dma_start(out=gain_sb[:], in_=gain)
+        nc.gpsimd.dma_start(out=og_sb[:], in_=og)
+
+        got_words_b = sb.tile([P, J], U16, name="got_words_b", align_bytes=64)
+        got_plane_b = sb.tile([P, J], U8, name="got_plane_b", align_bytes=64)
+        nc.vector.tensor_copy(got_words_b[:], words_b[:].indirect(list_b[:]))
+        nc.vector.tensor_copy(got_plane_b[:], plane_b[:].indirect(list_b[:]))
+
+        w2o_bf = sb.tile([P, 2 * R * PACK], BF16, name="w2o_bf", align_bytes=64)
+        w2o_codes = sb.tile([P, 2 * R], U32, name="w2o_codes", align_bytes=64)
+        w2o_plane = sb.tile([P, 2 * R], U8, name="w2o_plane", align_bytes=64)
+        interleave(nc, w2o_bf[:, : R * PACK], w2_raw[:])
+        interleave(nc, w2o_bf[:, R * PACK :], wo_raw[:])
+        nc.vector.quantize_mx(out=w2o_codes[:].bitcast(FP8X4), scales=w2o_plane[:], in_=w2o_bf[:])
+
+        b_ps = ps.tile([P, J], F32, name="b_ps")
+        nc.tensor.matmul_mx(
+            out=b_ps[:], lhsT=w2o_codes[:, :R].bitcast(FP8X4), lhsT_scale=w2o_plane[:, :R],
+            rhs=got_words_b[:].bitcast(FP4X4), rhs_scale=got_plane_b[:], start=True, stop=True,
+        )
+
+        dy_bf = sb.tile([P, M * PACK], BF16, name="dy_bf", align_bytes=64)
+        dy_codes = sb.tile([P, M], U32, name="dy_codes", align_bytes=64)
+        dy_plane = sb.tile([P, M], U8, name="dy_plane", align_bytes=64)
+        interleave(nc, dy_bf[:], dy_raw[:])
+
+        g1 = sb.tile([P, J], F32, name="g1")
+        nc.scalar.activation(out=g1[:], in_=b_ps[:], func=ACT.Sigmoid)
+
+        got_words_a = sb.tile([P, J], U16, name="got_words_a", align_bytes=64)
+        got_plane_a = sb.tile([P, J], U8, name="got_plane_a", align_bytes=64)
+        nc.vector.quantize_mx(out=dy_codes[:].bitcast(FP8X4), scales=dy_plane[:], in_=dy_bf[:])
+        nc.vector.tensor_copy(got_words_a[:], words_a[:].indirect(list_a[:]))
+        c_ps = ps.tile([P, M], F32, name="c_ps")
+        nc.tensor.matmul_mx(
+            out=c_ps[:], lhsT=w2o_codes[:, R:].bitcast(FP8X4), lhsT_scale=w2o_plane[:, R:],
+            rhs=dy_codes[:].bitcast(FP8X4), rhs_scale=dy_plane[:], start=True, stop=True,
+        )
+        nc.vector.tensor_copy(got_plane_a[:], plane_a[:].indirect(list_a[:]))
+
+        w1_bf = sb.tile([P, R * PACK], BF16, name="w1_bf", align_bytes=64)
+        w1_codes = sb.tile([P, R], U32, name="w1_codes", align_bytes=64)
+        w1_plane = sb.tile([P, R], U8, name="w1_plane", align_bytes=64)
+        c_gain = sb.tile([P, M], F32, name="c_gain")
+        nc.scalar.activation(out=c_gain[:], in_=c_ps[:], func=ACT.Copy, scale=gain_sb[:])
+        interleave(nc, w1_bf[:], w1_raw[:])
+        nc.vector.quantize_mx(out=w1_codes[:].bitcast(FP8X4), scales=w1_plane[:], in_=w1_bf[:])
+        a_ps = ps.tile([P, J], F32, name="a_ps")
+        nc.tensor.matmul_mx(
+            out=a_ps[:], lhsT=w1_codes[:].bitcast(FP8X4), lhsT_scale=w1_plane[:],
+            rhs=got_words_a[:].bitcast(FP4X4), rhs_scale=got_plane_a[:], start=True, stop=True,
+        )
+
+        picked = sb.tile([P, M], F32, name="picked")
+        nc.vector.tensor_tensor(picked[:], g1[:].indirect(list_gate[:]), c_gain[:], ALU.mult)
+        nc.vector.tensor_tensor(placed[:].indirect(list_put[:]), picked[:], picked[:], ALU.mult)
+
+        h0 = sb.tile([P, J], F32, name="h0")
+        h_sq = sb.tile([P, J], F32, name="h_sq")
+        slope_sq = sb.tile([P, J], F32, name="slope_sq")
+        nc.scalar.activation(out=h0[:], in_=a_ps[:], func=ACT.Tanh)
+        nc.scalar.activation(out=h_sq[:], in_=h0[:], func=ACT.Square)
+        nc.scalar.activation(out=slope_sq[:], in_=h_sq[:], func=ACT.Square, scale=-1.0, bias=1.0)
+
+        factor = sb.tile([P, J], F32, name="factor")
+        nc.vector.scalar_tensor_tensor(factor[:], h0[:], og_sb[:], slope_sq[:], ALU.mult, ALU.mult)
+        prod = sb.tile([P, J], F32, name="prod")
+        res = sb.tile([P, J], F32, name="res")
+        half = J // HALVES
+        for i in range(HALVES):
+            cols = slice(i * half, (i + 1) * half)
+            nc.vector.tensor_tensor(prod[:, cols], placed[:, cols], factor[:, cols], ALU.mult)
+        for i in range(HALVES):
+            cols = slice(i * half, (i + 1) * half)
+            nc.vector.scalar_tensor_tensor(res[:, cols], prod[:, cols], -4.0, base_sb[:, cols], ALU.mult, ALU.add)
+            nc.sync.dma_start(out=out[:, cols], in_=res[:, cols])

@@ -54,7 +54,7 @@ def tile_attend_gpcpickgates_kernel(
         words_b = sb.tile([P, T], U16, name="words_b", align_bytes=64)
         plane_a = sb.tile([P, T], U8, name="plane_a", align_bytes=64)
         plane_b = sb.tile([P, T], U8, name="plane_b", align_bytes=64)
-        w1_raw = sb.tile([P, PACK, R], F32, name="w1_raw")
+        w1_raw = sb.tile([P, PACK, R], F32, name="w1_raw", tag="w1_then_g1")
         w2_raw = sb.tile([P, PACK, R], F32, name="w2_raw")
         wo_raw = sb.tile([P, PACK, R], F32, name="wo_raw")
         dy_raw = sb.tile([P, PACK, M], F32, name="dy_raw")
@@ -72,70 +72,73 @@ def tile_attend_gpcpickgates_kernel(
 
         nc.sync.dma_start(list_b[:], offs4)
         nc.sync.dma_start(out=words_b[:].bitcast(I32), in_=tab2_words[0].bitcast(I32))
-        load_scale_rows(nc.scalar, plane_b, tab2_scales)
-        nc.scalar.activation(out=warm_out[:], in_=warm_in[:], func=ACT.Sigmoid)
-        nc.sync.dma_start(out=w2_raw[:], in_=w2.rearrange("(p t) r -> p t r", t=PACK))
-        nc.sync.dma_start(out=wo_raw[:], in_=wo.rearrange("(p t) r -> p t r", t=PACK))
-        nc.sync.dma_start(out=dy_raw[:], in_=dy.rearrange("(p t) m -> p t m", t=PACK))
-        nc.sync.dma_start(out=words_a[:].bitcast(I32), in_=tab_words[0].bitcast(I32))
         nc.sync.dma_start(list_a[:], offs)
+        nc.sync.dma_start(out=w2_raw[:], in_=w2.rearrange("(p t) r -> p t r", t=PACK))
+        load_scale_rows(nc.sync, plane_b, tab2_scales)
+        nc.sync.dma_start(out=dy_raw[:], in_=dy.rearrange("(p t) m -> p t m", t=PACK))
+        nc.sync.dma_start(out=wo_raw[:], in_=wo.rearrange("(p t) r -> p t r", t=PACK))
         load_scale_rows(nc.sync, plane_a, tab_scales)
         nc.sync.dma_start(out=w1_raw[:], in_=w1.rearrange("(p t) r -> p t r", t=PACK))
+        nc.sync.dma_start(out=words_a[:].bitcast(I32), in_=tab_words[0].bitcast(I32))
         nc.sync.dma_start(list_gate[:], offs3)
         nc.sync.dma_start(list_put[:], offs2)
         nc.sync.dma_start(out=base_sb[:], in_=base)
         nc.gpsimd.dma_start(out=gain_sb[:], in_=gain)
         nc.gpsimd.dma_start(out=og_sb[:], in_=og)
+        nc.scalar.activation(out=warm_out[:], in_=warm_in[:], func=ACT.Sigmoid)
 
         got_words_b = sb.tile([P, J], U16, name="got_words_b", align_bytes=64)
         got_plane_b = sb.tile([P, J], U8, name="got_plane_b", align_bytes=64)
         nc.vector.tensor_copy(got_words_b[:], words_b[:].indirect(list_b[:]))
         nc.vector.tensor_copy(got_plane_b[:], plane_b[:].indirect(list_b[:]))
 
-        w2o_bf = sb.tile([P, 2 * R * PACK], BF16, name="w2o_bf", align_bytes=64)
-        w2o_codes = sb.tile([P, 2 * R], U32, name="w2o_codes", align_bytes=64)
-        w2o_plane = sb.tile([P, 2 * R], U8, name="w2o_plane", align_bytes=64)
-        interleave(nc, w2o_bf[:, : R * PACK], w2_raw[:])
-        interleave(nc, w2o_bf[:, R * PACK :], wo_raw[:])
-        nc.vector.quantize_mx(out=w2o_codes[:].bitcast(FP8X4), scales=w2o_plane[:], in_=w2o_bf[:])
-
+        w2_bf = sb.tile([P, R * PACK], BF16, name="w2_bf", align_bytes=64)
+        w2_codes = sb.tile([P, R], U32, name="w2_codes", align_bytes=64)
+        w2_plane = sb.tile([P, R], U8, name="w2_plane", align_bytes=64)
+        interleave(nc, w2_bf[:], w2_raw[:])
+        nc.vector.quantize_mx(out=w2_codes[:].bitcast(FP8X4), scales=w2_plane[:], in_=w2_bf[:])
         b_ps = ps.tile([P, J], F32, name="b_ps")
         nc.tensor.matmul_mx(
-            out=b_ps[:], lhsT=w2o_codes[:, :R].bitcast(FP8X4), lhsT_scale=w2o_plane[:, :R],
+            out=b_ps[:], lhsT=w2_codes[:].bitcast(FP8X4), lhsT_scale=w2_plane[:],
             rhs=got_words_b[:].bitcast(FP4X4), rhs_scale=got_plane_b[:], start=True, stop=True,
         )
+
+        got_words_a = sb.tile([P, J], U16, name="got_words_a", align_bytes=64)
+        got_plane_a = sb.tile([P, J], U8, name="got_plane_a", align_bytes=64)
+        nc.vector.tensor_copy(got_plane_a[:], plane_a[:].indirect(list_a[:]))
 
         dy_bf = sb.tile([P, M * PACK], BF16, name="dy_bf", align_bytes=64)
         dy_codes = sb.tile([P, M], U32, name="dy_codes", align_bytes=64)
         dy_plane = sb.tile([P, M], U8, name="dy_plane", align_bytes=64)
         interleave(nc, dy_bf[:], dy_raw[:])
-
-        g1 = sb.tile([P, J], F32, name="g1")
-        nc.scalar.activation(out=g1[:], in_=b_ps[:], func=ACT.Sigmoid)
-
-        got_words_a = sb.tile([P, J], U16, name="got_words_a", align_bytes=64)
-        got_plane_a = sb.tile([P, J], U8, name="got_plane_a", align_bytes=64)
         nc.vector.quantize_mx(out=dy_codes[:].bitcast(FP8X4), scales=dy_plane[:], in_=dy_bf[:])
-        nc.vector.tensor_copy(got_words_a[:], words_a[:].indirect(list_a[:]))
+
+        wo1_bf = sb.tile([P, 2 * R * PACK], BF16, name="wo1_bf", align_bytes=64)
+        wo1_codes = sb.tile([P, 2 * R], U32, name="wo1_codes", align_bytes=64)
+        wo1_plane = sb.tile([P, 2 * R], U8, name="wo1_plane", align_bytes=64)
+        interleave(nc, wo1_bf[:, : R * PACK], wo_raw[:])
+        interleave(nc, wo1_bf[:, R * PACK :], w1_raw[:])
+        nc.vector.quantize_mx(out=wo1_codes[:].bitcast(FP8X4), scales=wo1_plane[:], in_=wo1_bf[:])
         c_ps = ps.tile([P, M], F32, name="c_ps")
         nc.tensor.matmul_mx(
-            out=c_ps[:], lhsT=w2o_codes[:, R:].bitcast(FP8X4), lhsT_scale=w2o_plane[:, R:],
+            out=c_ps[:], lhsT=wo1_codes[:, :R].bitcast(FP8X4), lhsT_scale=wo1_plane[:, :R],
             rhs=dy_codes[:].bitcast(FP8X4), rhs_scale=dy_plane[:], start=True, stop=True,
         )
-        nc.vector.tensor_copy(got_plane_a[:], plane_a[:].indirect(list_a[:]))
 
-        w1_bf = sb.tile([P, R * PACK], BF16, name="w1_bf", align_bytes=64)
-        w1_codes = sb.tile([P, R], U32, name="w1_codes", align_bytes=64)
-        w1_plane = sb.tile([P, R], U8, name="w1_plane", align_bytes=64)
+        g1 = sb.tile([P, J], F32, name="g1", tag="w1_then_g1")
+        nc.scalar.activation(out=g1[:], in_=b_ps[:], func=ACT.Sigmoid)
         c_gain = sb.tile([P, M], F32, name="c_gain")
         nc.scalar.activation(out=c_gain[:], in_=c_ps[:], func=ACT.Copy, scale=gain_sb[:])
-        interleave(nc, w1_bf[:], w1_raw[:])
-        nc.vector.quantize_mx(out=w1_codes[:].bitcast(FP8X4), scales=w1_plane[:], in_=w1_bf[:])
-        a_ps = ps.tile([P, J], F32, name="a_ps")
-        nc.tensor.matmul_mx(
-            out=a_ps[:], lhsT=w1_codes[:].bitcast(FP8X4), lhsT_scale=w1_plane[:],
-            rhs=got_words_a[:].bitcast(FP4X4), rhs_scale=got_plane_a[:], start=True, stop=True,
-        )
+
+        halves = [slice(i * J // HALVES, (i + 1) * J // HALVES) for i in range(HALVES)]
+        a_ps = [ps.tile([P, J // HALVES], F32, name="a_ps%d" % i) for i in range(HALVES)]
+        for i, cols in enumerate(halves):
+            entries = slice(cols.start // 16, cols.stop // 16)
+            nc.vector.tensor_copy(got_words_a[:, cols], words_a[:].indirect(list_a[:, entries]))
+            nc.tensor.matmul_mx(
+                out=a_ps[i][:], lhsT=wo1_codes[:, R:].bitcast(FP8X4), lhsT_scale=wo1_plane[:, R:],
+                rhs=got_words_a[:, cols].bitcast(FP4X4), rhs_scale=got_plane_a[:, cols], start=True, stop=True,
+            )
 
         picked = sb.tile([P, M], F32, name="picked")
         nc.vector.tensor_tensor(picked[:], g1[:].indirect(list_gate[:]), c_gain[:], ALU.mult)
@@ -144,19 +147,20 @@ def tile_attend_gpcpickgates_kernel(
         h0 = sb.tile([P, J], F32, name="h0")
         h_sq = sb.tile([P, J], F32, name="h_sq")
         slope_sq = sb.tile([P, J], F32, name="slope_sq")
-        nc.scalar.activation(out=h0[:], in_=a_ps[:], func=ACT.Tanh)
-        nc.scalar.activation(out=h_sq[:], in_=h0[:], func=ACT.Square)
-        nc.scalar.activation(out=slope_sq[:], in_=h_sq[:], func=ACT.Square, scale=-1.0, bias=1.0)
+        for i, cols in enumerate(halves):
+            nc.scalar.activation(out=h0[:, cols], in_=a_ps[i][:], func=ACT.Tanh)
+        for cols in halves:
+            nc.scalar.activation(out=h_sq[:, cols], in_=h0[:, cols], func=ACT.Square)
+        for cols in halves:
+            nc.scalar.activation(out=slope_sq[:, cols], in_=h_sq[:, cols], func=ACT.Square, scale=-1.0, bias=1.0)
 
-        factor = sb.tile([P, J], F32, name="factor")
-        nc.vector.scalar_tensor_tensor(factor[:], h0[:], og_sb[:], slope_sq[:], ALU.mult, ALU.mult)
-        prod = sb.tile([P, J], F32, name="prod")
+        with_h = sb.tile([P, J], F32, name="with_h")
+        with_slope = sb.tile([P, J], F32, name="with_slope")
         res = sb.tile([P, J], F32, name="res")
-        half = J // HALVES
-        for i in range(HALVES):
-            cols = slice(i * half, (i + 1) * half)
-            nc.vector.tensor_tensor(prod[:, cols], placed[:, cols], factor[:, cols], ALU.mult)
-        for i in range(HALVES):
-            cols = slice(i * half, (i + 1) * half)
-            nc.vector.scalar_tensor_tensor(res[:, cols], prod[:, cols], -4.0, base_sb[:, cols], ALU.mult, ALU.add)
+        for cols in halves:
+            nc.vector.scalar_tensor_tensor(with_h[:, cols], placed[:, cols], og_sb[:], h0[:, cols], ALU.mult, ALU.mult)
+        for cols in halves:
+            nc.vector.tensor_tensor(with_slope[:, cols], with_h[:, cols], slope_sq[:, cols], ALU.mult)
+        for cols in halves:
+            nc.vector.scalar_tensor_tensor(res[:, cols], with_slope[:, cols], -4.0, base_sb[:, cols], ALU.mult, ALU.add)
             nc.sync.dma_start(out=out[:, cols], in_=res[:, cols])

@@ -31,10 +31,10 @@ def interleave(nc, grouped, raw):
 
 
 def load_scale_rows(queue, plane, scales):
-    for q in range(QUADS):
+    for i in range(QUADS):
         queue.dma_start(
-            out=plane[32 * q : 32 * q + 4, :].bitcast(I32),
-            in_=scales[0, 4 * q : 4 * q + 4, :].bitcast(I32),
+            out=plane[i:P:32, :].bitcast(I32),
+            in_=scales[0, i:16:QUADS, :].bitcast(I32),
         )
 
 
@@ -52,12 +52,12 @@ def tile_attend_gpcpickgates_kernel(
         list_gate = sb.tile([P, M // 16], U16, name="list_gate")
         words_a = sb.tile([P, T], U16, name="words_a", align_bytes=64)
         words_b = sb.tile([P, T], U16, name="words_b", align_bytes=64)
-        plane_a = sb.tile([P, T], U8, name="plane_a", align_bytes=64)
+        plane_a = sb.tile([P, T], U8, name="plane_a", tag="plane_a_then_codes", align_bytes=64)
         plane_b = sb.tile([P, T], U8, name="plane_b", align_bytes=64)
         w1_raw = sb.tile([P, PACK, R], F32, name="w1_raw", tag="w1_then_g1")
         w2_raw = sb.tile([P, PACK, R], F32, name="w2_raw")
         wo_raw = sb.tile([P, PACK, R], F32, name="wo_raw")
-        dy_raw = sb.tile([P, PACK, M], F32, name="dy_raw")
+        dy_raw = sb.tile([P, PACK, M], F32, name="dy_raw", tag="dy_then_bf", align_bytes=64)
         base_sb = sb.tile([P, J], F32, name="base_sb")
         gain_sb = sb.tile([P, 1], F32, name="gain_sb")
         og_sb = sb.tile([P, 1], F32, name="og_sb")
@@ -82,9 +82,9 @@ def tile_attend_gpcpickgates_kernel(
         nc.sync.dma_start(out=words_a[:].bitcast(I32), in_=tab_words[0].bitcast(I32))
         nc.sync.dma_start(list_gate[:], offs3)
         nc.sync.dma_start(list_put[:], offs2)
+        nc.sync.dma_start(out=gain_sb[:], in_=gain)
+        nc.sync.dma_start(out=og_sb[:], in_=og)
         nc.sync.dma_start(out=base_sb[:], in_=base)
-        nc.gpsimd.dma_start(out=gain_sb[:], in_=gain)
-        nc.gpsimd.dma_start(out=og_sb[:], in_=og)
         nc.scalar.activation(out=warm_out[:], in_=warm_in[:], func=ACT.Sigmoid)
 
         got_words_b = sb.tile([P, J], U16, name="got_words_b", align_bytes=64)
@@ -108,12 +108,12 @@ def tile_attend_gpcpickgates_kernel(
         nc.vector.tensor_copy(got_plane_a[:], plane_a[:].indirect(list_a[:]))
 
         dy_bf = sb.tile([P, M * PACK], BF16, name="dy_bf", align_bytes=64)
-        dy_codes = sb.tile([P, M], U32, name="dy_codes", align_bytes=64)
+        dy_codes = sb.tile([P, M], U32, name="dy_codes", tag="plane_a_then_codes", align_bytes=64)
         dy_plane = sb.tile([P, M], U8, name="dy_plane", align_bytes=64)
         interleave(nc, dy_bf[:], dy_raw[:])
         nc.vector.quantize_mx(out=dy_codes[:].bitcast(FP8X4), scales=dy_plane[:], in_=dy_bf[:])
 
-        wo1_bf = sb.tile([P, 2 * R * PACK], BF16, name="wo1_bf", align_bytes=64)
+        wo1_bf = sb.tile([P, 2 * R * PACK], BF16, name="wo1_bf", tag="dy_then_bf", align_bytes=64)
         wo1_codes = sb.tile([P, 2 * R], U32, name="wo1_codes", align_bytes=64)
         wo1_plane = sb.tile([P, 2 * R], U8, name="wo1_plane", align_bytes=64)
         interleave(nc, wo1_bf[:, : R * PACK], wo_raw[:])
@@ -128,7 +128,7 @@ def tile_attend_gpcpickgates_kernel(
         g1 = sb.tile([P, J], F32, name="g1", tag="w1_then_g1")
         nc.scalar.activation(out=g1[:], in_=b_ps[:], func=ACT.Sigmoid)
         c_gain = sb.tile([P, M], F32, name="c_gain")
-        nc.scalar.activation(out=c_gain[:], in_=c_ps[:], func=ACT.Copy, scale=gain_sb[:])
+        nc.scalar.copy(out=c_gain[:], in_=c_ps[:])
 
         halves = [slice(i * J // HALVES, (i + 1) * J // HALVES) for i in range(HALVES)]
         a_ps = [ps.tile([P, J // HALVES], F32, name="a_ps%d" % i) for i in range(HALVES)]
@@ -144,6 +144,8 @@ def tile_attend_gpcpickgates_kernel(
         nc.vector.tensor_tensor(picked[:], g1[:].indirect(list_gate[:]), c_gain[:], ALU.mult)
         nc.vector.tensor_tensor(placed[:].indirect(list_put[:]), picked[:], picked[:], ALU.mult)
 
+        neg_gain = sb.tile([P, 1], F32, name="neg_gain")
+        nc.gpsimd.tensor_scalar_mul(neg_gain[:], gain_sb[:], -1.0)
         h0 = sb.tile([P, J], F32, name="h0")
         h_sq = sb.tile([P, J], F32, name="h_sq")
         slope_sq = sb.tile([P, J], F32, name="slope_sq")
@@ -152,15 +154,15 @@ def tile_attend_gpcpickgates_kernel(
         for cols in halves:
             nc.scalar.activation(out=h_sq[:, cols], in_=h0[:, cols], func=ACT.Square)
         for cols in halves:
-            nc.scalar.activation(out=slope_sq[:, cols], in_=h_sq[:, cols], func=ACT.Square, scale=-1.0, bias=1.0)
+            nc.scalar.activation(out=slope_sq[:, cols], in_=h_sq[:, cols], func=ACT.Square, scale=neg_gain[:], bias=gain_sb[:])
 
-        with_h = sb.tile([P, J], F32, name="with_h")
-        with_slope = sb.tile([P, J], F32, name="with_slope")
+        factor = sb.tile([P, J], F32, name="factor")
+        prod = sb.tile([P, J], F32, name="prod")
         res = sb.tile([P, J], F32, name="res")
         for cols in halves:
-            nc.vector.scalar_tensor_tensor(with_h[:, cols], placed[:, cols], og_sb[:], h0[:, cols], ALU.mult, ALU.mult)
+            nc.vector.scalar_tensor_tensor(factor[:, cols], h0[:, cols], og_sb[:], slope_sq[:, cols], ALU.mult, ALU.mult)
         for cols in halves:
-            nc.vector.tensor_tensor(with_slope[:, cols], with_h[:, cols], slope_sq[:, cols], ALU.mult)
+            nc.vector.tensor_tensor(prod[:, cols], placed[:, cols], factor[:, cols], ALU.mult)
         for cols in halves:
-            nc.vector.scalar_tensor_tensor(res[:, cols], with_slope[:, cols], -4.0, base_sb[:, cols], ALU.mult, ALU.add)
+            nc.vector.scalar_tensor_tensor(res[:, cols], prod[:, cols], -4.0, base_sb[:, cols], ALU.mult, ALU.add)
             nc.sync.dma_start(out=out[:, cols], in_=res[:, cols])

from contextlib import ExitStack

import concourse.mybir as mybir

K, R, F, T, J, M = 512, 128, 512, 2048, 512, 256
FLOPS = 2 * K * R * J * 2 + 2 * F * R * M

F32 = mybir.dt.float32
BF16 = mybir.dt.bfloat16
I32 = mybir.dt.int32
U32 = mybir.dt.uint32
U16 = mybir.dt.uint16
U8 = mybir.dt.uint8
FP8X4 = mybir.dt.float8_e4m3fn_x4
FP4X4 = mybir.dt.float4_e2m1fn_x4
ACT = mybir.ActivationFunctionType
ALU = mybir.AluOpType

P = 128
PACK = 4
LINE = 4
QUADS = 4
HALVES = 2


def interleave(nc, grouped, raw):
    nc.scalar.copy(
        out=grouped.rearrange("p (c i t) -> p c t i", i=LINE, t=PACK),
        in_=raw.rearrange("p t (c i) -> p c t i", i=LINE),
    )


def load_scale_rows(queue, plane, scales):
    for i in range(QUADS):
        queue.dma_start(
            out=plane[i:P:32, :].bitcast(I32),
            in_=scales[0, i:16:QUADS, :].bitcast(I32),
        )


def tile_attend_gpcpickgates_kernel(
    tc, tab_words, tab_scales, w1, tab2_words, tab2_scales, w2, gain, wo, dy, og, base, offs, offs4, offs2, offs3, out
):
    nc = tc.nc
    with ExitStack() as ctx:
        sb = ctx.enter_context(tc.tile_pool(name="sb", bufs=1))
        ps = ctx.enter_context(tc.psum_pool(name="ps", bufs=1))

        list_a = sb.tile([P, J // 16], U16, name="list_a")
        list_b = sb.tile([P, J // 16], U16, name="list_b")
        list_put = sb.tile([P, M // 16], U16, name="list_put")
        list_gate = sb.tile([P, M // 16], U16, name="list_gate")
        words_a = sb.tile([P, T], U16, name="words_a", align_bytes=64)
        words_b = sb.tile([P, T], U16, name="words_b", align_bytes=64)
        plane_a = sb.tile([P, T], U8, name="plane_a", tag="plane_a_then_codes", align_bytes=64)
        plane_b = sb.tile([P, T], U8, name="plane_b", align_bytes=64)
        w1_raw = sb.tile([P, PACK, R], F32, name="w1_raw", tag="w1_then_g1")
        w2_raw = sb.tile([P, PACK, R], F32, name="w2_raw")
        wo_raw = sb.tile([P, PACK, R], F32, name="wo_raw")
        dy_raw = sb.tile([P, PACK, M], F32, name="dy_raw", tag="dy_then_bf", align_bytes=64)
        base_sb = sb.tile([P, J], F32, name="base_sb")
        gain_sb = sb.tile([P, 1], F32, name="gain_sb")
        og_sb = sb.tile([P, 1], F32, name="og_sb")
        placed = sb.tile([P, J], F32, name="placed")
        warm_in = sb.tile([P, 1], F32, name="warm_in")
        warm_out = sb.tile([P, 1], F32, name="warm_out")

        nc.vector.memset(plane_b[:].bitcast(I32), 0)
        nc.vector.memset(plane_a[:].bitcast(I32), 0)
        nc.vector.memset(placed[:], 0.0)
        nc.gpsimd.memset(warm_in[:], 0.0)

        nc.sync.dma_start(list_b[:], offs4)
        nc.sync.dma_start(out=words_b[:].bitcast(I32), in_=tab2_words[0].bitcast(I32))
        nc.sync.dma_start(list_a[:], offs)
        nc.sync.dma_start(out=w2_raw[:], in_=w2.rearrange("(p t) r -> p t r", t=PACK))
        load_scale_rows(nc.sync, plane_b, tab2_scales)
        nc.sync.dma_start(out=dy_raw[:], in_=dy.rearrange("(p t) m -> p t m", t=PACK))
        nc.sync.dma_start(out=wo_raw[:], in_=wo.rearrange("(p t) r -> p t r", t=PACK))
        load_scale_rows(nc.sync, plane_a, tab_scales)
        nc.sync.dma_start(out=w1_raw[:], in_=w1.rearrange("(p t) r -> p t r", t=PACK))
        nc.sync.dma_start(out=words_a[:].bitcast(I32), in_=tab_words[0].bitcast(I32))
        nc.sync.dma_start(list_gate[:], offs3)
        nc.sync.dma_start(list_put[:], offs2)
        nc.sync.dma_start(out=gain_sb[:], in_=gain)
        nc.sync.dma_start(out=og_sb[:], in_=og)
        nc.sync.dma_start(out=base_sb[:], in_=base)
        nc.scalar.activation(out=warm_out[:], in_=warm_in[:], func=ACT.Sigmoid)

        got_words_b = sb.tile([P, J], U16, name="got_words_b", align_bytes=64)
        got_plane_b = sb.tile([P, J], U8, name="got_plane_b", align_bytes=64)
        nc.vector.tensor_copy(got_words_b[:], words_b[:].indirect(list_b[:]))
        nc.vector.tensor_copy(got_plane_b[:], plane_b[:].indirect(list_b[:]))

        w2_bf = sb.tile([P, R * PACK], BF16, name="w2_bf", align_bytes=64)
        w2_codes = sb.tile([P, R], U32, name="w2_codes", align_bytes=64)
        w2_plane = sb.tile([P, R], U8, name="w2_plane", align_bytes=64)
        interleave(nc, w2_bf[:], w2_raw[:])
        nc.vector.quantize_mx(out=w2_codes[:].bitcast(FP8X4), scales=w2_plane[:], in_=w2_bf[:])
        b_ps = ps.tile([P, J], F32, name="b_ps")
        nc.tensor.matmul_mx(
            out=b_ps[:], lhsT=w2_codes[:].bitcast(FP8X4), lhsT_scale=w2_plane[:],
            rhs=got_words_b[:].bitcast(FP4X4), rhs_scale=got_plane_b[:], start=True, stop=True,
        )

        got_words_a = sb.tile([P, J], U16, name="got_words_a", align_bytes=64)
        got_plane_a = sb.tile([P, J], U8, name="got_plane_a", align_bytes=64)
        nc.vector.tensor_copy(got_plane_a[:], plane_a[:].indirect(list_a[:]))

        dy_bf = sb.tile([P, M * PACK], BF16, name="dy_bf", align_bytes=64)
        dy_codes = sb.tile([P, M], U32, name="dy_codes", tag="plane_a_then_codes", align_bytes=64)
        dy_plane = sb.tile([P, M], U8, name="dy_plane", align_bytes=64)
        interleave(nc, dy_bf[:], dy_raw[:])
        nc.vector.quantize_mx(out=dy_codes[:].bitcast(FP8X4), scales=dy_plane[:], in_=dy_bf[:])

        wo1_bf = sb.tile([P, 2 * R * PACK], BF16, name="wo1_bf", tag="dy_then_bf", align_bytes=64)
        wo1_codes = sb.tile([P, 2 * R], U32, name="wo1_codes", align_bytes=64)
        wo1_plane = sb.tile([P, 2 * R], U8, name="wo1_plane", align_bytes=64)
        interleave(nc, wo1_bf[:, : R * PACK], wo_raw[:])
        interleave(nc, wo1_bf[:, R * PACK :], w1_raw[:])
        nc.vector.quantize_mx(out=wo1_codes[:].bitcast(FP8X4), scales=wo1_plane[:], in_=wo1_bf[:])
        c_ps = ps.tile([P, M], F32, name="c_ps")
        nc.tensor.matmul_mx(
            out=c_ps[:], lhsT=wo1_codes[:, :R].bitcast(FP8X4), lhsT_scale=wo1_plane[:, :R],
            rhs=dy_codes[:].bitcast(FP8X4), rhs_scale=dy_plane[:], start=True, stop=True,
        )

        g1 = sb.tile([P, J], F32, name="g1", tag="w1_then_g1")
        nc.scalar.activation(out=g1[:], in_=b_ps[:], func=ACT.Sigmoid)
        c_gain = sb.tile([P, M], F32, name="c_gain")
        nc.scalar.copy(out=c_gain[:], in_=c_ps[:])

        halves = [slice(i * J // HALVES, (i + 1) * J // HALVES) for i in range(HALVES)]
        a_ps = [ps.tile([P, J // HALVES], F32, name="a_ps%d" % i) for i in range(HALVES)]
        for i, cols in enumerate(halves):
            entries = slice(cols.start // 16, cols.stop // 16)
            nc.vector.tensor_copy(got_words_a[:, cols], words_a[:].indirect(list_a[:, entries]))
            nc.tensor.matmul_mx(
                out=a_ps[i][:], lhsT=wo1_codes[:, R:].bitcast(FP8X4), lhsT_scale=wo1_plane[:, R:],
                rhs=got_words_a[:, cols].bitcast(FP4X4), rhs_scale=got_plane_a[:, cols], start=True, stop=True,
            )

        picked = sb.tile([P, M], F32, name="picked")
        nc.vector.tensor_tensor(picked[:], g1[:].indirect(list_gate[:]), c_gain[:], ALU.mult)
        nc.vector.tensor_tensor(placed[:].indirect(list_put[:]), picked[:], picked[:], ALU.mult)

        neg_gain = sb.tile([P, 1], F32, name="neg_gain")
        nc.gpsimd.tensor_scalar_mul(neg_gain[:], gain_sb[:], -1.0)
        h0 = sb.tile([P, J], F32, name="h0")
        h_sq = sb.tile([P, J], F32, name="h_sq")
        slope_sq = sb.tile([P, J], F32, name="slope_sq")
        for i, cols in enumerate(halves):
            nc.scalar.activation(out=h0[:, cols], in_=a_ps[i][:], func=ACT.Tanh)
        for cols in halves:
            nc.scalar.activation(out=h_sq[:, cols], in_=h0[:, cols], func=ACT.Square)
        for cols in halves:
            nc.scalar.activation(out=slope_sq[:, cols], in_=h_sq[:, cols], func=ACT.Square, scale=neg_gain[:], bias=gain_sb[:])

        factor = sb.tile([P, J], F32, name="factor")
        prod = sb.tile([P, J], F32, name="prod")
        res = sb.tile([P, J], F32, name="res")
        for cols in halves:
            nc.vector.scalar_tensor_tensor(factor[:, cols], h0[:, cols], og_sb[:], slope_sq[:, cols], ALU.mult, ALU.mult)
        for cols in halves:
            nc.vector.tensor_tensor(prod[:, cols], placed[:, cols], factor[:, cols], ALU.mult)
        for cols in halves:
            nc.vector.scalar_tensor_tensor(res[:, cols], prod[:, cols], -4.0, base_sb[:, cols], ALU.mult, ALU.add)
            nc.sync.dma_start(out=out[:, cols], in_=res[:, cols])
